import numpy as np
import ml_dtypes


def mxq(x, axis, fmt="e4m3"):
    dtype, down = {"e4m3": (ml_dtypes.float8_e4m3fn, 7), "e5m2": (ml_dtypes.float8_e5m2, 14)}[fmt]
    v = np.moveaxis(np.asarray(x, np.float32).astype(ml_dtypes.bfloat16).astype(np.float64), axis, -1)
    blocks = v.reshape(v.shape[:-1] + (-1, 32))
    amax = np.abs(blocks).max(-1, keepdims=True)
    byte = np.maximum(np.where(amax > 0, np.frexp(amax)[1] - 1 + 127, 0) - down, 1)
    scale = np.exp2(byte - 127.0)
    codes = (blocks / scale).astype(np.float32).astype(dtype).astype(np.float64)
    return np.moveaxis((codes * scale).reshape(v.shape), -1, axis)


WIDE = False


def mx_kscale(k):
    if not WIDE:
        return np.ones(k)
    levels = np.array([10, -10, 5, -5, 0])
    if k % 512:
        return np.exp2(np.random.permutation(np.resize(levels, k // 32))).repeat(32)
    a = np.empty((k // 512, 16))
    for p in range(k // 512):
        a[p, :8] = np.random.permutation(np.resize(levels, 8))
        for g in range(8):
            far = levels[np.abs(levels - a[p, g]) >= 10]
            a[p, g + 8] = far[np.random.randint(len(far))]
    return np.exp2(a.ravel()).repeat(32)


BF16 = ml_dtypes.bfloat16


def bf(x):
    return np.asarray(x, np.float32).astype(BF16)


def f64(x):
    return np.asarray(x).astype(np.float64)


E2M1 = np.array([0.0, 0.5, 1.0, 1.5, 2.0, 3.0, 4.0, 6.0, -0.0, -0.5, -1.0, -1.5, -2.0, -3.0, -4.0, -6.0])


def pack_weight(w, fmt):
    k, n = w.shape
    w = f64(bf(w)).reshape(k // 32, 32, n)
    amax = np.abs(w).max(1)
    if fmt == "e4m3":
        byte = np.frexp(amax)[1] - 1 + 127 - 7
    else:
        mant, ex = np.frexp(amax / 6.0)
        byte = np.where(mant > 0.5, ex, ex - 1) + 127
    byte = np.clip(np.where(amax > 0, byte, 1), 1, 254)
    scaled = (w * np.exp2(127.0 - byte)[:, None, :]).reshape(k, n).astype(np.float32)
    by_word = np.ascontiguousarray(scaled.reshape(k // 512, 128, 4, n).transpose(0, 1, 3, 2))
    if fmt == "e4m3":
        words = by_word.astype(ml_dtypes.float8_e4m3fn).view(np.uint8)
    else:
        c = by_word.astype(ml_dtypes.float4_e2m1fn).view(np.uint8) & 0xF
        words = c[..., 0::2] | (c[..., 1::2] << 4)
    return np.ascontiguousarray(words), np.ascontiguousarray(byte.astype(np.uint8).reshape(k // 512, 16, n))


def unpack_weight(words, scales, fmt):
    g, p, n, _ = words.shape
    if fmt == "e4m3":
        vals = np.ascontiguousarray(words).view(ml_dtypes.float8_e4m3fn).astype(np.float64)
    else:
        nib = np.empty((g, p, n, 4), np.uint8)
        nib[..., 0::2] = words & 0xF
        nib[..., 1::2] = words >> 4
        vals = E2M1[nib]
    vals = vals * np.repeat(np.exp2(scales.astype(np.float64) - 127.0), 8, axis=1)[..., None]
    return vals.transpose(0, 1, 3, 2).reshape(g * 512, n)
def pack4(w):
    words, scales = pack_weight(w, "e2m1")
    return words.reshape(words.shape[0], 128, -1), scales


def unpack4(words, scales):
    return unpack_weight(words.reshape(words.shape[0], 128, -1, 2), scales, "e2m1")


L, M, CD, CE, S, P = 4, 512, 512, 2048, 1024, 4096


def setup_inputs():
    s, u, t = mx_kscale(CD), mx_kscale(CE), mx_kscale(S)
    gd = np.random.standard_normal((M, CD)) + np.random.standard_normal((L, M, CD))
    ge = np.random.standard_normal((M, CE)) + np.random.standard_normal((L, M, CE))
    deep = np.random.standard_normal((CD, S)) / s[:, None] * t
    early = np.random.standard_normal((CE, S)) / u[:, None] * t
    up = np.random.standard_normal((S, P)) / np.sqrt(S) / t[:, None]
    early_words, early_scales = pack4(early)
    up_words, up_scales = pack4(up)
    return {"grad_deep": bf(gd / np.sqrt(CD) * s),
            "grad_early": bf(ge / np.sqrt(CE) * u),
            "deep": bf(deep),
            "early_words": early_words, "early_scales": early_scales,
            "up_words": up_words, "up_scales": up_scales}


def reference(grad_deep, grad_early, deep, early_words, early_scales, up_words, up_scales):
    a_deep = f64(grad_deep).mean(0)
    a_early = f64(grad_early).mean(0)
    z = ((mxq(a_deep, 1, "e4m3") @ mxq(f64(deep), 0, "e4m3"))
         + (mxq(a_early, 1, "e4m3") @ unpack4(early_words, early_scales)))
    cam = np.maximum(z, 0.0)
    return mxq(cam, 1, "e4m3") @ unpack4(up_words, up_scales)

@@ -1,0 +1,298 @@
+from contextlib import ExitStack
+
+import concourse.mybir as mybir
+from concourse.masks import make_identity
+
+F32 = mybir.dt.float32
+BF16 = mybir.dt.bfloat16
+I32 = mybir.dt.int32
+U32 = mybir.dt.uint32
+U8 = mybir.dt.uint8
+FP8X4 = mybir.dt.float8_e4m3fn_x4
+FP4X4 = mybir.dt.float4_e2m1fn_x4
+RELU = mybir.ActivationFunctionType.Relu
+
+P = 128
+L, M, CD, CE, S, NPIX = 4, 512, 512, 2048, 1024, 4096
+K = 512
+JT = M // P
+GE = CE // K
+GS = S // K
+NT = NPIX // 512
+FLOPS = 2 * M * (CD + CE) * S + 2 * M * S * NPIX
+GROUPS = ((0,), (1, 2), (3, 4))
+
+
+def tile_two_layer_gradcam_s3_kernel(
+    tc, grad_deep, grad_early, deep, early_words, early_scales, up_words, up_scales, out
+):
+    nc = tc.nc
+    gd_view = grad_deep.rearrange("l (i j) k -> (l i) j k", j=16)
+    ge_view = grad_early.rearrange("l (i j) k -> (l i) j k", j=16)
+    out_view = out.rearrange("(i j) n -> j i n", j=16)
+
+    with ExitStack() as ctx:
+        keep = ctx.enter_context(tc.tile_pool(name="keep", bufs=1))
+        grads = ctx.enter_context(tc.tile_pool(name="grads", bufs=3))
+        work = ctx.enter_context(tc.tile_pool(name="work", bufs=2))
+        outs = ctx.enter_context(tc.tile_pool(name="outs", bufs=8))
+        psum = ctx.enter_context(tc.psum_pool(name="psum", bufs=2))
+
+        ident = keep.tile([P, P], F32, align_bytes=64)
+        deep_raw = keep.tile([P, 4, S], BF16, align_bytes=64)
+        deep_grouped = keep.tile([P, S * 4], BF16, align_bytes=64)
+        deep_codes = keep.tile([P, S], U32, align_bytes=64)
+        deep_scales = keep.tile([P, S], U8, align_bytes=64)
+        ew = keep.tile([P, GE, 2 * S], U8, align_bytes=64)
+        es = keep.tile([P, GE, S], U8, align_bytes=64)
+        uw = keep.tile([P, GS, 2 * NPIX], U8, align_bytes=64)
+        us = keep.tile([P, GS, NPIX], U8, align_bytes=64)
+        warm = keep.tile([P, 1], F32)
+        gd = [keep.tile([P, 8, CD], BF16, name="gd%d" % h, align_bytes=64) for h in range(2)]
+        pick = keep.tile([P, 32], BF16, align_bytes=64)
+        ge = {}
+
+        ctx.enter_context(tc.manual_schedule())
+
+        def load_ge(J, half):
+            if half == 0:
+                ge[J] = [grads.tile([P, 4 * CE // 2], BF16, name="ge%d" % i, align_bytes=64) for i in range(2)]
+            t = ge[J][half]
+            if J == 0:
+                dst = t[:].rearrange("p (j k) -> p j k", j=4)
+                nc.sync.dma_start(out=dst, in_=ge_view[:, 0:4, half * 1024 : (half + 1) * 1024])
+            else:
+                dst = t[:].rearrange("p (j k) -> p j k", j=2)
+                nc.sync.dma_start(out=dst, in_=ge_view[:, 4 * J + 2 * half : 4 * J + 2 * half + 2, :])
+
+        def load_gd(h):
+            nc.sync.dma_start(out=gd[h][:], in_=gd_view[:, 8 * h : 8 * h + 8, :])
+
+        def load_scales(plane, rows, groups):
+            for r in range(4):
+                nc.sync.dma_start(
+                    out=plane[r:P:32, :, :].bitcast(I32),
+                    in_=rows.rearrange("g (q r) n -> r q g n", r=4)[r].bitcast(I32),
+                )
+
+        nc.vector.memset(warm[:], 0.0)
+        nc.scalar.activation(out=warm[:], in_=warm[:], func=RELU)
+        nc.gpsimd.memset(es[:].rearrange("p g n -> p (g n)").bitcast(I32), 0)
+        make_identity(nc, ident[:])
+        for l in range(L):
+            nc.vector.tensor_copy(out=pick[32 * l : 32 * l + 32, :], in_=ident[32 * l : 32 * l + 32, 32 * l : 32 * l + 32])
+        nc.gpsimd.memset(us[:].rearrange("p g n -> p (g n)").bitcast(I32), 0)
+
+        def load_ew(h):
+            nc.sync.dma_start(
+                out=ew[:, 2 * h : 2 * h + 2, :].bitcast(I32),
+                in_=early_words[2 * h : 2 * h + 2].rearrange("g p n -> p g n").bitcast(I32),
+            )
+
+        def load_uw(h):
+            nc.sync.dma_start(
+                out=uw[:, :, h * NPIX : (h + 1) * NPIX].bitcast(I32),
+                in_=up_words[:, :, h * NPIX : (h + 1) * NPIX].rearrange("g p n -> p g n").bitcast(I32),
+            )
+
+        nc.sync.dma_start(out=deep_raw[:], in_=deep.rearrange("(p j) w -> p j w", j=4))
+        load_gd(0)
+        load_ge(0, 0)
+        load_scales(es, early_scales, GE)
+        load_scales(us, up_scales, GS)
+        load_ew(0)
+        load_ge(0, 1)
+        load_ew(1)
+        load_ge(1, 0)
+        load_uw(0)
+        load_ge(1, 1)
+        load_uw(1)
+        load_gd(1)
+        load_ge(2, 0)
+        load_ge(2, 1)
+
+        half = S // 2
+        for h, eng in ((0, nc.vector.tensor_copy), (1, nc.scalar.copy)):
+            eng(
+                out=deep_grouped[:, h * half * 4 : (h + 1) * half * 4].rearrange("p (w j) -> p w j", j=4),
+                in_=deep_raw[:, :, h * half : (h + 1) * half].rearrange("p j w -> p w j"),
+            )
+
+        def quantize_deep(h):
+            nc.vector.quantize_mx(
+                out=deep_codes[:, h * half : (h + 1) * half].bitcast(FP8X4),
+                scales=deep_scales[:, h * half : (h + 1) * half],
+                in_=deep_grouped[:, h * half * 4 : (h + 1) * half * 4],
+            )
+
+        st = {}
+
+        def rows(J, jj, u, t):
+            if u == 0:
+                return gd[J // 2][:, (J % 2) * 4 + jj, t:CD:4]
+            if J == 0:
+                base = jj * 1024 + ((u - 1) % 2) * K
+                return ge[J][(u - 1) // 2][:, base + t : base + K : 4]
+            base = (jj % 2) * CE + (u - 1) * K
+            return ge[J][jj // 2][:, base + t : base + K : 4]
+
+        def begin(J):
+            st[J] = {
+                "ag": work.tile([P, 5 * K], BF16, name="ag", align_bytes=64),
+                "ac": work.tile([P, 5 * P], U32, name="ac", align_bytes=64),
+                "as": work.tile([P, 5 * P], U8, name="a_s", align_bytes=64),
+                "sum": {},
+            }
+
+        def sum_cells(J, u):
+            acc = psum.tile([P, K], F32, name="b", bufs=6)
+            for t in range(4):
+                for jj in range(4):
+                    nc.tensor.matmul(
+                        acc[:, t * P + 32 * jj : t * P + 32 * jj + 32], lhsT=rows(J, jj, u, t), rhs=pick[:], start=True, stop=True
+                    )
+            nc.vector.tensor_scalar(
+                out=st[J]["ag"][:, u * K : (u + 1) * K].rearrange("p (i j t) -> p i j t", j=4, t=4),
+                in0=acc[:].rearrange("p (t j i) -> p i j t", t=4, j=4),
+                scalar1=0.25,
+                scalar2=None,
+                op0=mybir.AluOpType.mult,
+            )
+
+        def quantize_a(J, g):
+            n = len(GROUPS[g])
+            u0 = GROUPS[g][0]
+            nc.vector.quantize_mx(
+                out=st[J]["ac"][:, u0 * P : (u0 + n) * P].bitcast(FP8X4),
+                scales=st[J]["as"][:, u0 * P : (u0 + n) * P],
+                in_=st[J]["ag"][:, u0 * K : (u0 + n) * K],
+            )
+
+        def stage1(J, units):
+            if units[0] == 0:
+                st[J]["z"] = [psum.tile([P, K], F32, name="z%d" % h, bufs=1) for h in range(2)]
+            for h in range(2):
+                for u in units:
+                    cols = slice(u * P, (u + 1) * P)
+                    if u == 0:
+                        rhs = deep_codes[:, h * K : (h + 1) * K].bitcast(FP8X4)
+                        rs = deep_scales[:, h * K : (h + 1) * K]
+                    else:
+                        rhs = ew[:, u - 1, h * 2 * K : (h + 1) * 2 * K].bitcast(FP4X4)
+                        rs = es[:, u - 1, h * K : (h + 1) * K]
+                    nc.tensor.matmul_mx(
+                        out=st[J]["z"][h][:],
+                        lhsT=st[J]["ac"][:, cols].bitcast(FP8X4),
+                        lhsT_scale=st[J]["as"][:, cols],
+                        rhs=rhs,
+                        rhs_scale=rs,
+                        start=(u == 0),
+                        stop=(u == 4),
+                    )
+
+        def relu(J):
+            st[J]["cam"] = work.tile([P, S], BF16, name="cam", align_bytes=64)
+            for h in range(2):
+                nc.scalar.activation(
+                    out=st[J]["cam"][:, h * K : (h + 1) * K].rearrange("m (u q e) -> m u q e", u=2, e=2),
+                    in_=st[J]["z"][h][:].rearrange("m (q u e) -> m u q e", u=2, e=2),
+                    func=RELU,
+                )
+
+        def cam_transposes(J):
+            tr = psum.tile([P, K], F32, name="b", bufs=6)
+            words = st[J]["cam"][:].bitcast(F32)
+            for i in range(4):
+                nc.tensor.transpose(tr[:, i * P : (i + 1) * P], words[:, i * P : (i + 1) * P], ident[:])
+            st[J]["ct"] = tr
+
+        def empty_cam(J):
+            st[J]["cg"] = work.tile([P, S], BF16, name="cg", align_bytes=64)
+            nc.scalar.copy(
+                out=st[J]["cg"][:].bitcast(F32).rearrange("p (c m v) -> p c m v", c=2, v=2),
+                in_=st[J]["ct"][:].rearrange("p (c v m) -> p c m v", c=2, v=2),
+            )
+
+        def quantize_cam(J):
+            st[J]["cc"] = work.tile([P, GS * P], U32, name="cc", align_bytes=64)
+            st[J]["cs"] = work.tile([P, GS * P], U8, name="cs", align_bytes=64)
+            nc.vector.quantize_mx(out=st[J]["cc"][:].bitcast(FP8X4), scales=st[J]["cs"][:], in_=st[J]["cg"][:])
+
+        def stage2(J, n):
+            o = psum.tile([P, 512], F32, name="b", bufs=6)
+            for g in range(GS):
+                nc.tensor.matmul_mx(
+                    out=o[:],
+                    lhsT=st[J]["cc"][:, g * P : (g + 1) * P].bitcast(FP8X4),
+                    lhsT_scale=st[J]["cs"][:, g * P : (g + 1) * P],
+                    rhs=uw[:, g, n * 1024 : (n + 1) * 1024].bitcast(FP4X4),
+                    rhs_scale=us[:, g, n * 512 : (n + 1) * 512],
+                    start=(g == 0),
+                    stop=(g == GS - 1),
+                )
+            if n % 4 == 0:
+                st[J]["o"] = outs.tile([P, 2048], F32, name="ot")
+            dst = st[J]["o"][:, (n % 4) * 512 : (n % 4 + 1) * 512]
+            if (J == JT - 1 or (J == JT - 2 and n > 4)) and n % 2 == 1:
+                nc.vector.tensor_copy(out=dst, in_=o[:])
+            else:
+                nc.scalar.copy(out=dst, in_=o[:])
+            if n % 4 == 3:
+                for jj in range(4):
+                    nc.sync.dma_start(
+                        out=out_view[4 * J + jj][:, (n - 3) * 512 : (n + 1) * 512], in_=st[J]["o"][jj:P:4, :]
+                    )
+
+        def back(J, ns):
+            if J >= 0:
+                for n in ns:
+                    stage2(J, n)
+
+        begin(0)
+        sum_cells(0, 0)
+        quantize_deep(0)
+        quantize_a(0, 0)
+        quantize_deep(1)
+        sum_cells(0, 1)
+        sum_cells(0, 2)
+        stage1(0, (0,))
+        quantize_a(0, 1)
+        stage1(0, (1, 2))
+        sum_cells(0, 3)
+        sum_cells(0, 4)
+        begin(1)
+        sum_cells(1, 0)
+        quantize_a(0, 2)
+        quantize_a(1, 0)
+        stage1(0, (3, 4))
+        load_ge(3, 0)
+        load_ge(3, 1)
+
+        for J in range(JT):
+            N = J + 1
+            if J > 0:
+                stage1(J, range(5))
+            relu(J)
+            if N < JT:
+                if N > 1:
+                    begin(N)
+                    sum_cells(N, 0)
+                sum_cells(N, 1)
+                sum_cells(N, 2)
+            else:
+                back(J - 1, (4,))
+            cam_transposes(J)
+            empty_cam(J)
+            quantize_cam(J)
+            if N < JT:
+                if N > 1:
+                    quantize_a(N, 0)
+                quantize_a(N, 1)
+                back(J - 1, (4,))
+            back(J - 1, (5, 6, 7))
+            if N < JT:
+                sum_cells(N, 3)
+                sum_cells(N, 4)
+                quantize_a(N, 2)
+            back(J, (0, 1, 2, 3))
+        back(JT - 1, (4, 5, 6, 7))

@@ -35,7 +35,7 @@ def tile_two_layer_gradcam_s3_kernel(
         keep = ctx.enter_context(tc.tile_pool(name="keep", bufs=1))
         grads = ctx.enter_context(tc.tile_pool(name="grads", bufs=3))
         work = ctx.enter_context(tc.tile_pool(name="work", bufs=2))
-        outs = ctx.enter_context(tc.tile_pool(name="outs", bufs=8))
+        outs = ctx.enter_context(tc.tile_pool(name="outs", bufs=4))
         psum = ctx.enter_context(tc.psum_pool(name="psum", bufs=2))
 
         ident = keep.tile([P, P], F32, align_bytes=64)
@@ -45,10 +45,10 @@ def tile_two_layer_gradcam_s3_kernel(
         deep_scales = keep.tile([P, S], U8, align_bytes=64)
         ew = keep.tile([P, GE, 2 * S], U8, align_bytes=64)
         es = keep.tile([P, GE, S], U8, align_bytes=64)
-        uw = keep.tile([P, GS, 2 * NPIX], U8, align_bytes=64)
+        uw = [keep.tile([P, GS, NPIX], U8, name="uw%d" % h, align_bytes=64) for h in range(2)]
         us = keep.tile([P, GS, NPIX], U8, align_bytes=64)
         warm = keep.tile([P, 1], F32)
-        gd = [keep.tile([P, 8, CD], BF16, name="gd%d" % h, align_bytes=64) for h in range(2)]
+        gd = [keep.tile([P, 4, CD], BF16, name="gd%d" % J, align_bytes=64) for J in range(JT)]
         pick = keep.tile([P, 32], BF16, align_bytes=64)
         ge = {}
 
@@ -65,23 +65,25 @@ def tile_two_layer_gradcam_s3_kernel(
                 dst = t[:].rearrange("p (j k) -> p j k", j=2)
                 nc.sync.dma_start(out=dst, in_=ge_view[:, 4 * J + 2 * half : 4 * J + 2 * half + 2, :])
 
-        def load_gd(h):
-            nc.sync.dma_start(out=gd[h][:], in_=gd_view[:, 8 * h : 8 * h + 8, :])
+        def load_gd(J):
+            nc.sync.dma_start(out=gd[J][:], in_=gd_view[:, 4 * J : 4 * J + 4, :])
 
         def load_scales(plane, rows, groups):
             for r in range(4):
-                nc.sync.dma_start(
+                nc.gpsimd.dma_start(
                     out=plane[r:P:32, :, :].bitcast(I32),
                     in_=rows.rearrange("g (q r) n -> r q g n", r=4)[r].bitcast(I32),
                 )
 
+        nc.vector.memset(es[:].rearrange("p g n -> p (g n)").bitcast(I32), 0)
+        nc.vector.memset(us[:].rearrange("p g n -> p (g n)").bitcast(I32), 0)
         nc.vector.memset(warm[:], 0.0)
         nc.scalar.activation(out=warm[:], in_=warm[:], func=RELU)
-        nc.gpsimd.memset(es[:].rearrange("p g n -> p (g n)").bitcast(I32), 0)
         make_identity(nc, ident[:])
+        load_scales(es, early_scales, GE)
+        load_scales(us, up_scales, GS)
         for l in range(L):
             nc.vector.tensor_copy(out=pick[32 * l : 32 * l + 32, :], in_=ident[32 * l : 32 * l + 32, 32 * l : 32 * l + 32])
-        nc.gpsimd.memset(us[:].rearrange("p g n -> p (g n)").bitcast(I32), 0)
 
         def load_ew(h):
             nc.sync.dma_start(
@@ -91,25 +93,25 @@ def tile_two_layer_gradcam_s3_kernel(
 
         def load_uw(h):
             nc.sync.dma_start(
-                out=uw[:, :, h * NPIX : (h + 1) * NPIX].bitcast(I32),
+                out=uw[h][:].bitcast(I32),
                 in_=up_words[:, :, h * NPIX : (h + 1) * NPIX].rearrange("g p n -> p g n").bitcast(I32),
             )
 
         nc.sync.dma_start(out=deep_raw[:], in_=deep.rearrange("(p j) w -> p j w", j=4))
         load_gd(0)
         load_ge(0, 0)
-        load_scales(es, early_scales, GE)
-        load_scales(us, up_scales, GS)
         load_ew(0)
         load_ge(0, 1)
         load_ew(1)
-        load_ge(1, 0)
         load_uw(0)
+        load_gd(1)
+        load_ge(1, 0)
         load_ge(1, 1)
         load_uw(1)
-        load_gd(1)
+        load_gd(2)
         load_ge(2, 0)
         load_ge(2, 1)
+        load_gd(3)
 
         half = S // 2
         for h, eng in ((0, nc.vector.tensor_copy), (1, nc.scalar.copy)):
@@ -129,7 +131,7 @@ def tile_two_layer_gradcam_s3_kernel(
 
         def rows(J, jj, u, t):
             if u == 0:
-                return gd[J // 2][:, (J % 2) * 4 + jj, t:CD:4]
+                return gd[J][:, jj, t:CD:4]
             if J == 0:
                 base = jj * 1024 + ((u - 1) % 2) * K
                 return ge[J][(u - 1) // 2][:, base + t : base + K : 4]
@@ -144,20 +146,28 @@ def tile_two_layer_gradcam_s3_kernel(
                 "sum": {},
             }
 
-        def sum_cells(J, u):
-            acc = psum.tile([P, K], F32, name="b", bufs=6)
+        def sum_part(J, u, groups):
+            if u not in st[J]["sum"]:
+                st[J]["sum"][u] = psum.tile([P, K], F32, name="b", bufs=6)
+            acc = st[J]["sum"][u]
             for t in range(4):
-                for jj in range(4):
+                for jj in groups:
                     nc.tensor.matmul(
                         acc[:, t * P + 32 * jj : t * P + 32 * jj + 32], lhsT=rows(J, jj, u, t), rhs=pick[:], start=True, stop=True
                     )
+
+        def empty_sum(J, u):
             nc.vector.tensor_scalar(
                 out=st[J]["ag"][:, u * K : (u + 1) * K].rearrange("p (i j t) -> p i j t", j=4, t=4),
-                in0=acc[:].rearrange("p (t j i) -> p i j t", t=4, j=4),
+                in0=st[J]["sum"][u][:].rearrange("p (t j i) -> p i j t", t=4, j=4),
                 scalar1=0.25,
                 scalar2=None,
                 op0=mybir.AluOpType.mult,
             )
+
+        def sum_cells(J, u):
+            sum_part(J, u, range(4))
+            empty_sum(J, u)
 
         def quantize_a(J, g):
             n = len(GROUPS[g])
@@ -225,7 +235,7 @@ def tile_two_layer_gradcam_s3_kernel(
                     out=o[:],
                     lhsT=st[J]["cc"][:, g * P : (g + 1) * P].bitcast(FP8X4),
                     lhsT_scale=st[J]["cs"][:, g * P : (g + 1) * P],
-                    rhs=uw[:, g, n * 1024 : (n + 1) * 1024].bitcast(FP4X4),
+                    rhs=uw[n // 4][:, g, (n % 4) * 1024 : (n % 4 + 1) * 1024].bitcast(FP4X4),
                     rhs_scale=us[:, g, n * 512 : (n + 1) * 512],
                     start=(g == 0),
                     stop=(g == GS - 1),
@@ -237,10 +247,13 @@ def tile_two_layer_gradcam_s3_kernel(
                 nc.vector.tensor_copy(out=dst, in_=o[:])
             else:
                 nc.scalar.copy(out=dst, in_=o[:])
-            if n % 4 == 3:
+            w = 2 if J == JT - 1 and n > 3 else 4
+            if n % w == w - 1:
+                lo = (n % 4 + 1 - w) * 512
                 for jj in range(4):
                     nc.sync.dma_start(
-                        out=out_view[4 * J + jj][:, (n - 3) * 512 : (n + 1) * 512], in_=st[J]["o"][jj:P:4, :]
+                        out=out_view[4 * J + jj][:, (n + 1 - w) * 512 : (n + 1) * 512],
+                        in_=st[J]["o"][jj:P:4, lo : lo + w * 512],
                     )
 
         def back(J, ns):
@@ -260,39 +273,59 @@ def tile_two_layer_gradcam_s3_kernel(
         stage1(0, (1, 2))
         sum_cells(0, 3)
         sum_cells(0, 4)
-        begin(1)
-        sum_cells(1, 0)
         quantize_a(0, 2)
-        quantize_a(1, 0)
         stage1(0, (3, 4))
+        relu(0)
         load_ge(3, 0)
         load_ge(3, 1)
+        begin(1)
+        sum_cells(1, 0)
+        quantize_a(1, 0)
+        cam_transposes(0)
+        empty_cam(0)
+        quantize_cam(0)
+        back(0, (0, 1, 2, 3))
+        for u in range(1, 5):
+            sum_part(1, u, (0, 1))
+        for u in range(1, 5):
+            sum_part(1, u, (2, 3))
+            empty_sum(1, u)
+            if u % 2 == 0:
+                quantize_a(1, u // 2)
+        back(0, (4, 5))
 
-        for J in range(JT):
+        for J in range(1, JT):
             N = J + 1
-            if J > 0:
-                stage1(J, range(5))
+            stage1(J, range(5))
             relu(J)
             if N < JT:
-                if N > 1:
-                    begin(N)
+                begin(N)
+                if J == 1:
+                    back(0, (6, 7))
+                    cam_transposes(J)
+                    empty_cam(J)
+                    quantize_cam(J)
                     sum_cells(N, 0)
-                sum_cells(N, 1)
-                sum_cells(N, 2)
-            else:
-                back(J - 1, (4,))
-            cam_transposes(J)
-            empty_cam(J)
-            quantize_cam(J)
-            if N < JT:
-                if N > 1:
-                    quantize_a(N, 0)
+                    sum_cells(N, 1)
+                    sum_cells(N, 2)
+                else:
+                    sum_cells(N, 0)
+                    sum_cells(N, 1)
+                    sum_cells(N, 2)
+                    cam_transposes(J)
+                    empty_cam(J)
+                    quantize_cam(J)
+                    back(J - 1, (4, 5, 6, 7))
+                quantize_a(N, 0)
                 quantize_a(N, 1)
-                back(J - 1, (4,))
-            back(J - 1, (5, 6, 7))
-            if N < JT:
                 sum_cells(N, 3)
                 sum_cells(N, 4)
                 quantize_a(N, 2)
+            else:
+                back(J - 1, (4, 5))
+                cam_transposes(J)
+                empty_cam(J)
+                quantize_cam(J)
+                back(J - 1, (6, 7))
             back(J, (0, 1, 2, 3))
         back(JT - 1, (4, 5, 6, 7))

@@ -58,19 +58,15 @@ def tile_two_layer_gradcam_s3_kernel(
             if half == 0:
                 ge[J] = [grads.tile([P, 4 * CE // 2], BF16, name="ge%d" % i, align_bytes=64) for i in range(2)]
             t = ge[J][half]
-            if J == 0:
-                dst = t[:].rearrange("p (j k) -> p j k", j=4)
-                nc.sync.dma_start(out=dst, in_=ge_view[:, 0:4, half * 1024 : (half + 1) * 1024])
-            else:
-                dst = t[:].rearrange("p (j k) -> p j k", j=2)
-                nc.sync.dma_start(out=dst, in_=ge_view[:, 4 * J + 2 * half : 4 * J + 2 * half + 2, :])
+            dst = t[:].rearrange("p (j k) -> p j k", j=2)
+            nc.sync.dma_start(out=dst, in_=ge_view[:, 4 * J + 2 * half : 4 * J + 2 * half + 2, :])
 
         def load_gd(J):
             nc.sync.dma_start(out=gd[J][:], in_=gd_view[:, 4 * J : 4 * J + 4, :])
 
         def load_scales(plane, rows, groups):
             for r in range(4):
-                nc.gpsimd.dma_start(
+                nc.sync.dma_start(
                     out=plane[r:P:32, :, :].bitcast(I32),
                     in_=rows.rearrange("g (q r) n -> r q g n", r=4)[r].bitcast(I32),
                 )
@@ -80,8 +76,6 @@ def tile_two_layer_gradcam_s3_kernel(
         nc.vector.memset(warm[:], 0.0)
         nc.scalar.activation(out=warm[:], in_=warm[:], func=RELU)
         make_identity(nc, ident[:])
-        load_scales(es, early_scales, GE)
-        load_scales(us, up_scales, GS)
         for l in range(L):
             nc.vector.tensor_copy(out=pick[32 * l : 32 * l + 32, :], in_=ident[32 * l : 32 * l + 32, 32 * l : 32 * l + 32])
 
@@ -97,28 +91,32 @@ def tile_two_layer_gradcam_s3_kernel(
                 in_=up_words[:, :, h * NPIX : (h + 1) * NPIX].rearrange("g p n -> p g n").bitcast(I32),
             )
 
-        nc.sync.dma_start(out=deep_raw[:], in_=deep.rearrange("(p j) w -> p j w", j=4))
+        half = S // 2
+
+        def deep_copies():
+            for h, eng in ((0, nc.vector.tensor_copy), (1, nc.scalar.copy)):
+                eng(
+                    out=deep_grouped[:, h * half * 4 : (h + 1) * half * 4].rearrange("p (w j) -> p w j", j=4),
+                    in_=deep_raw[:, :, h * half : (h + 1) * half].rearrange("p j w -> p w j"),
+                )
+
         load_gd(0)
         load_ge(0, 0)
-        load_ew(0)
+        nc.sync.dma_start(out=deep_raw[:], in_=deep.rearrange("(p j) w -> p j w", j=4))
         load_ge(0, 1)
+        load_scales(es, early_scales, GE)
+        load_ew(0)
         load_ew(1)
-        load_uw(0)
         load_gd(1)
         load_ge(1, 0)
         load_ge(1, 1)
-        load_uw(1)
+        load_scales(us, up_scales, GS)
+        load_uw(0)
         load_gd(2)
         load_ge(2, 0)
+        load_uw(1)
         load_ge(2, 1)
         load_gd(3)
-
-        half = S // 2
-        for h, eng in ((0, nc.vector.tensor_copy), (1, nc.scalar.copy)):
-            eng(
-                out=deep_grouped[:, h * half * 4 : (h + 1) * half * 4].rearrange("p (w j) -> p w j", j=4),
-                in_=deep_raw[:, :, h * half : (h + 1) * half].rearrange("p j w -> p w j"),
-            )
 
         def quantize_deep(h):
             nc.vector.quantize_mx(
@@ -132,9 +130,6 @@ def tile_two_layer_gradcam_s3_kernel(
         def rows(J, jj, u, t):
             if u == 0:
                 return gd[J][:, jj, t:CD:4]
-            if J == 0:
-                base = jj * 1024 + ((u - 1) % 2) * K
-                return ge[J][(u - 1) // 2][:, base + t : base + K : 4]
             base = (jj % 2) * CE + (u - 1) * K
             return ge[J][jj // 2][:, base + t : base + K : 4]
 
@@ -143,6 +138,7 @@ def tile_two_layer_gradcam_s3_kernel(
                 "ag": work.tile([P, 5 * K], BF16, name="ag", align_bytes=64),
                 "ac": work.tile([P, 5 * P], U32, name="ac", align_bytes=64),
                 "as": work.tile([P, 5 * P], U8, name="a_s", align_bytes=64),
+                "n": 0,
                 "sum": {},
             }
 
@@ -247,7 +243,7 @@ def tile_two_layer_gradcam_s3_kernel(
                 nc.vector.tensor_copy(out=dst, in_=o[:])
             else:
                 nc.scalar.copy(out=dst, in_=o[:])
-            w = 2 if J == JT - 1 and n > 3 else 4
+            w = 2 if J > 1 and n > 3 else 4
             if n % w == w - 1:
                 lo = (n % 4 + 1 - w) * 512
                 for jj in range(4):
@@ -256,24 +252,33 @@ def tile_two_layer_gradcam_s3_kernel(
                         in_=st[J]["o"][jj:P:4, lo : lo + w * 512],
                     )
 
-        def back(J, ns):
-            if J >= 0:
-                for n in ns:
-                    stage2(J, n)
+        def back(J, count):
+            for n in range(st[J]["n"], st[J]["n"] + count):
+                stage2(J, n)
+            st[J]["n"] += count
+
+        def halves(J, us_):
+            for u in us_:
+                sum_part(J, u, (0, 1))
+
+        def finish(J, us_):
+            for u in us_:
+                sum_part(J, u, (2, 3))
+                empty_sum(J, u)
 
         begin(0)
         sum_cells(0, 0)
-        quantize_deep(0)
+        deep_copies()
         quantize_a(0, 0)
+        quantize_deep(0)
+        halves(0, (1, 2, 3, 4))
+        finish(0, (1, 2))
         quantize_deep(1)
-        sum_cells(0, 1)
-        sum_cells(0, 2)
-        stage1(0, (0,))
         quantize_a(0, 1)
-        stage1(0, (1, 2))
-        sum_cells(0, 3)
-        sum_cells(0, 4)
+        finish(0, (3, 4))
+        stage1(0, (0,))
         quantize_a(0, 2)
+        stage1(0, (1, 2))
         stage1(0, (3, 4))
         relu(0)
         load_ge(3, 0)
@@ -284,48 +289,56 @@ def tile_two_layer_gradcam_s3_kernel(
         cam_transposes(0)
         empty_cam(0)
         quantize_cam(0)
-        back(0, (0, 1, 2, 3))
-        for u in range(1, 5):
-            sum_part(1, u, (0, 1))
-        for u in range(1, 5):
-            sum_part(1, u, (2, 3))
-            empty_sum(1, u)
+        halves(1, (1, 2, 3, 4))
+        finish(1, (1, 2))
+        quantize_a(1, 1)
+        finish(1, (3, 4))
+        quantize_a(1, 2)
+        stage1(1, (0,))
+        stage1(1, (1, 2))
+        back(0, 1)
+        stage1(1, (3, 4))
+        relu(1)
+        back(0, 1)
+        begin(2)
+        sum_cells(2, 0)
+        quantize_a(2, 0)
+        cam_transposes(1)
+        empty_cam(1)
+        quantize_cam(1)
+        back(0, 2)
+        stage1(2, (0,))
+        back(1, 4)
+        back(0, 4)
+        for u in (1, 2, 3, 4):
+            sum_cells(2, u)
             if u % 2 == 0:
-                quantize_a(1, u // 2)
-        back(0, (4, 5))
-
-        for J in range(1, JT):
-            N = J + 1
-            stage1(J, range(5))
-            relu(J)
-            if N < JT:
-                begin(N)
-                if J == 1:
-                    back(0, (6, 7))
-                    cam_transposes(J)
-                    empty_cam(J)
-                    quantize_cam(J)
-                    sum_cells(N, 0)
-                    sum_cells(N, 1)
-                    sum_cells(N, 2)
-                else:
-                    sum_cells(N, 0)
-                    sum_cells(N, 1)
-                    sum_cells(N, 2)
-                    cam_transposes(J)
-                    empty_cam(J)
-                    quantize_cam(J)
-                    back(J - 1, (4, 5, 6, 7))
-                quantize_a(N, 0)
-                quantize_a(N, 1)
-                sum_cells(N, 3)
-                sum_cells(N, 4)
-                quantize_a(N, 2)
-            else:
-                back(J - 1, (4, 5))
-                cam_transposes(J)
-                empty_cam(J)
-                quantize_cam(J)
-                back(J - 1, (6, 7))
-            back(J, (0, 1, 2, 3))
-        back(JT - 1, (4, 5, 6, 7))
+                quantize_a(2, u // 2)
+        begin(3)
+        sum_cells(3, 0)
+        quantize_a(3, 0)
+        back(1, 2)
+        stage1(2, (1, 2))
+        stage1(2, (3, 4))
+        relu(2)
+        sum_cells(3, 1)
+        sum_cells(3, 2)
+        back(1, 2)
+        cam_transposes(2)
+        empty_cam(2)
+        quantize_a(3, 1)
+        quantize_cam(2)
+        sum_cells(3, 3)
+        sum_cells(3, 4)
+        quantize_a(3, 2)
+        stage1(3, (0,))
+        stage1(3, (1, 2))
+        back(2, 2)
+        stage1(3, (3, 4))
+        relu(3)
+        back(2, 3)
+        cam_transposes(3)
+        empty_cam(3)
+        quantize_cam(3)
+        back(2, 3)
+        back(3, 8)

@@ -11,6 +11,7 @@ U8 = mybir.dt.uint8
 FP8X4 = mybir.dt.float8_e4m3fn_x4
 FP4X4 = mybir.dt.float4_e2m1fn_x4
 RELU = mybir.ActivationFunctionType.Relu
+COPY = mybir.ActivationFunctionType.Copy
 
 P = 128
 L, M, CD, CE, S, NPIX = 4, 512, 512, 2048, 1024, 4096
@@ -19,6 +20,7 @@ JT = M // P
 GE = CE // K
 GS = S // K
 NT = NPIX // 512
+SCALAR_SUMS = ((0, 2), (0, 4), (1, 2), (1, 4))
 FLOPS = 2 * M * (CD + CE) * S + 2 * M * S * NPIX
 GROUPS = ((0,), (1, 2), (3, 4))
 
@@ -27,9 +29,9 @@ def tile_two_layer_gradcam_s3_kernel(
     tc, grad_deep, grad_early, deep, early_words, early_scales, up_words, up_scales, out
 ):
     nc = tc.nc
-    gd_view = grad_deep.rearrange("l (i j) k -> (l i) j k", j=16)
-    ge_view = grad_early.rearrange("l (i j) k -> (l i) j k", j=16)
-    out_view = out.rearrange("(i j) n -> j i n", j=16)
+    gd_view = grad_deep.rearrange("l (i j c) k -> c (l i) j k", j=4, c=JT)
+    ge_view = grad_early.rearrange("l (i j c) k -> c (l i) j k", j=4, c=JT)
+    out_view = out.rearrange("(q c) n -> c q n", c=JT)
 
     with ExitStack() as ctx:
         keep = ctx.enter_context(tc.tile_pool(name="keep", bufs=1))
@@ -59,10 +61,10 @@ def tile_two_layer_gradcam_s3_kernel(
                 ge[J] = [grads.tile([P, 4 * CE // 2], BF16, name="ge%d" % i, align_bytes=64) for i in range(2)]
             t = ge[J][half]
             dst = t[:].rearrange("p (j k) -> p j k", j=2)
-            nc.sync.dma_start(out=dst, in_=ge_view[:, 4 * J + 2 * half : 4 * J + 2 * half + 2, :])
+            nc.sync.dma_start(out=dst, in_=ge_view[J][:, 2 * half : 2 * half + 2, :])
 
         def load_gd(J):
-            nc.sync.dma_start(out=gd[J][:], in_=gd_view[:, 4 * J : 4 * J + 4, :])
+            nc.sync.dma_start(out=gd[J][:], in_=gd_view[J])
 
         def load_scales(plane, rows, groups):
             for r in range(4):
@@ -153,13 +155,12 @@ def tile_two_layer_gradcam_s3_kernel(
                     )
 
         def empty_sum(J, u):
-            nc.vector.tensor_scalar(
-                out=st[J]["ag"][:, u * K : (u + 1) * K].rearrange("p (i j t) -> p i j t", j=4, t=4),
-                in0=st[J]["sum"][u][:].rearrange("p (t j i) -> p i j t", t=4, j=4),
-                scalar1=0.25,
-                scalar2=None,
-                op0=mybir.AluOpType.mult,
-            )
+            dst = st[J]["ag"][:, u * K : (u + 1) * K].rearrange("p (i j t) -> p i j t", j=4, t=4)
+            src = st[J]["sum"][u][:].rearrange("p (t j i) -> p i j t", t=4, j=4)
+            if (J, u) in SCALAR_SUMS:
+                nc.scalar.activation(out=dst, in_=src, func=COPY, scale=0.25)
+            else:
+                nc.vector.tensor_scalar(out=dst, in0=src, scalar1=0.25, scalar2=None, op0=mybir.AluOpType.mult)
 
         def sum_cells(J, u):
             sum_part(J, u, range(4))
@@ -243,14 +244,12 @@ def tile_two_layer_gradcam_s3_kernel(
                 nc.vector.tensor_copy(out=dst, in_=o[:])
             else:
                 nc.scalar.copy(out=dst, in_=o[:])
-            w = 2 if J > 1 and n > 3 else 4
+            w = 4 if J < 2 else 2 if J < 3 or n < 6 else 1
             if n % w == w - 1:
                 lo = (n % 4 + 1 - w) * 512
-                for jj in range(4):
-                    nc.sync.dma_start(
-                        out=out_view[4 * J + jj][:, (n + 1 - w) * 512 : (n + 1) * 512],
-                        in_=st[J]["o"][jj:P:4, lo : lo + w * 512],
-                    )
+                nc.sync.dma_start(
+                    out=out_view[J][:, (n + 1 - w) * 512 : (n + 1) * 512], in_=st[J]["o"][:, lo : lo + w * 512]
+                )
 
         def back(J, count):
             for n in range(st[J]["n"], st[J]["n"] + count):
@@ -296,10 +295,9 @@ def tile_two_layer_gradcam_s3_kernel(
         quantize_a(1, 2)
         stage1(1, (0,))
         stage1(1, (1, 2))
-        back(0, 1)
         stage1(1, (3, 4))
         relu(1)
-        back(0, 1)
+        back(0, 2)
         begin(2)
         sum_cells(2, 0)
         quantize_a(2, 0)
@@ -336,9 +334,9 @@ def tile_two_layer_gradcam_s3_kernel(
         back(2, 2)
         stage1(3, (3, 4))
         relu(3)
-        back(2, 3)
+        back(2, 4)
         cam_transposes(3)
         empty_cam(3)
         quantize_cam(3)
-        back(2, 3)
+        back(2, 2)
         back(3, 8)

from contextlib import ExitStack

import concourse.mybir as mybir
from concourse.masks import make_identity

F32 = mybir.dt.float32
BF16 = mybir.dt.bfloat16
I32 = mybir.dt.int32
U32 = mybir.dt.uint32
U8 = mybir.dt.uint8
FP8X4 = mybir.dt.float8_e4m3fn_x4
FP4X4 = mybir.dt.float4_e2m1fn_x4
RELU = mybir.ActivationFunctionType.Relu
COPY = mybir.ActivationFunctionType.Copy

P = 128
L, M, CD, CE, S, NPIX = 4, 512, 512, 2048, 1024, 4096
K = 512
JT = M // P
GE = CE // K
GS = S // K
NT = NPIX // 512
SCALAR_SUMS = ((0, 2), (0, 4), (1, 2), (1, 4))
FLOPS = 2 * M * (CD + CE) * S + 2 * M * S * NPIX
GROUPS = ((0,), (1, 2), (3, 4))


def tile_two_layer_gradcam_s3_kernel(
    tc, grad_deep, grad_early, deep, early_words, early_scales, up_words, up_scales, out
):
    nc = tc.nc
    gd_view = grad_deep.rearrange("l (i j c) k -> c (l i) j k", j=4, c=JT)
    ge_view = grad_early.rearrange("l (i j c) k -> c (l i) j k", j=4, c=JT)
    out_view = out.rearrange("(q c) n -> c q n", c=JT)

    with ExitStack() as ctx:
        keep = ctx.enter_context(tc.tile_pool(name="keep", bufs=1))
        grads = ctx.enter_context(tc.tile_pool(name="grads", bufs=3))
        work = ctx.enter_context(tc.tile_pool(name="work", bufs=2))
        outs = ctx.enter_context(tc.tile_pool(name="outs", bufs=4))
        psum = ctx.enter_context(tc.psum_pool(name="psum", bufs=2))

        ident = keep.tile([P, P], F32, align_bytes=64)
        deep_raw = keep.tile([P, 4, S], BF16, align_bytes=64)
        deep_grouped = keep.tile([P, S * 4], BF16, align_bytes=64)
        deep_codes = keep.tile([P, S], U32, align_bytes=64)
        deep_scales = keep.tile([P, S], U8, align_bytes=64)
        ew = keep.tile([P, GE, 2 * S], U8, align_bytes=64)
        es = keep.tile([P, GE, S], U8, align_bytes=64)
        uw = [keep.tile([P, GS, NPIX], U8, name="uw%d" % h, align_bytes=64) for h in range(2)]
        us = keep.tile([P, GS, NPIX], U8, align_bytes=64)
        warm = keep.tile([P, 1], F32)
        gd = [keep.tile([P, 4, CD], BF16, name="gd%d" % J, align_bytes=64) for J in range(JT)]
        pick = keep.tile([P, 32], BF16, align_bytes=64)
        ge = {}

        ctx.enter_context(tc.manual_schedule())

        def load_ge(J, half):
            if half == 0:
                ge[J] = [grads.tile([P, 4 * CE // 2], BF16, name="ge%d" % i, align_bytes=64) for i in range(2)]
            t = ge[J][half]
            dst = t[:].rearrange("p (j k) -> p j k", j=2)
            nc.sync.dma_start(out=dst, in_=ge_view[J][:, 2 * half : 2 * half + 2, :])

        def load_gd(J):
            nc.sync.dma_start(out=gd[J][:], in_=gd_view[J])

        def load_scales(plane, rows, groups):
            for r in range(4):
                nc.sync.dma_start(
                    out=plane[r:P:32, :, :].bitcast(I32),
                    in_=rows.rearrange("g (q r) n -> r q g n", r=4)[r].bitcast(I32),
                )

        nc.vector.memset(es[:].rearrange("p g n -> p (g n)").bitcast(I32), 0)
        nc.vector.memset(us[:].rearrange("p g n -> p (g n)").bitcast(I32), 0)
        nc.vector.memset(warm[:], 0.0)
        nc.scalar.activation(out=warm[:], in_=warm[:], func=RELU)
        make_identity(nc, ident[:])
        for l in range(L):
            nc.vector.tensor_copy(out=pick[32 * l : 32 * l + 32, :], in_=ident[32 * l : 32 * l + 32, 32 * l : 32 * l + 32])

        def load_ew(h):
            nc.sync.dma_start(
                out=ew[:, 2 * h : 2 * h + 2, :].bitcast(I32),
                in_=early_words[2 * h : 2 * h + 2].rearrange("g p n -> p g n").bitcast(I32),
            )

        def load_uw(h):
            nc.sync.dma_start(
                out=uw[h][:].bitcast(I32),
                in_=up_words[:, :, h * NPIX : (h + 1) * NPIX].rearrange("g p n -> p g n").bitcast(I32),
            )

        half = S // 2

        def deep_copies():
            for h, eng in ((0, nc.vector.tensor_copy), (1, nc.scalar.copy)):
                eng(
                    out=deep_grouped[:, h * half * 4 : (h + 1) * half * 4].rearrange("p (w j) -> p w j", j=4),
                    in_=deep_raw[:, :, h * half : (h + 1) * half].rearrange("p j w -> p w j"),
                )

        load_gd(0)
        load_ge(0, 0)
        nc.sync.dma_start(out=deep_raw[:], in_=deep.rearrange("(p j) w -> p j w", j=4))
        load_ge(0, 1)
        load_scales(es, early_scales, GE)
        load_ew(0)
        load_ew(1)
        load_gd(1)
        load_ge(1, 0)
        load_ge(1, 1)
        load_scales(us, up_scales, GS)
        load_uw(0)
        load_gd(2)
        load_ge(2, 0)
        load_uw(1)
        load_ge(2, 1)
        load_gd(3)

        def quantize_deep(h):
            nc.vector.quantize_mx(
                out=deep_codes[:, h * half : (h + 1) * half].bitcast(FP8X4),
                scales=deep_scales[:, h * half : (h + 1) * half],
                in_=deep_grouped[:, h * half * 4 : (h + 1) * half * 4],
            )

        st = {}

        def rows(J, jj, u, t):
            if u == 0:
                return gd[J][:, jj, t:CD:4]
            base = (jj % 2) * CE + (u - 1) * K
            return ge[J][jj // 2][:, base + t : base + K : 4]

        def begin(J):
            st[J] = {
                "ag": work.tile([P, 5 * K], BF16, name="ag", align_bytes=64),
                "ac": work.tile([P, 5 * P], U32, name="ac", align_bytes=64),
                "as": work.tile([P, 5 * P], U8, name="a_s", align_bytes=64),
                "n": 0,
                "sum": {},
            }

        def sum_part(J, u, groups):
            if u not in st[J]["sum"]:
                st[J]["sum"][u] = psum.tile([P, K], F32, name="b", bufs=6)
            acc = st[J]["sum"][u]
            for t in range(4):
                for jj in groups:
                    nc.tensor.matmul(
                        acc[:, t * P + 32 * jj : t * P + 32 * jj + 32], lhsT=rows(J, jj, u, t), rhs=pick[:], start=True, stop=True
                    )

        def empty_sum(J, u):
            dst = st[J]["ag"][:, u * K : (u + 1) * K].rearrange("p (i j t) -> p i j t", j=4, t=4)
            src = st[J]["sum"][u][:].rearrange("p (t j i) -> p i j t", t=4, j=4)
            if (J, u) in SCALAR_SUMS:
                nc.scalar.activation(out=dst, in_=src, func=COPY, scale=0.25)
            else:
                nc.vector.tensor_scalar(out=dst, in0=src, scalar1=0.25, scalar2=None, op0=mybir.AluOpType.mult)

        def sum_cells(J, u):
            sum_part(J, u, range(4))
            empty_sum(J, u)

        def quantize_a(J, g):
            n = len(GROUPS[g])
            u0 = GROUPS[g][0]
            nc.vector.quantize_mx(
                out=st[J]["ac"][:, u0 * P : (u0 + n) * P].bitcast(FP8X4),
                scales=st[J]["as"][:, u0 * P : (u0 + n) * P],
                in_=st[J]["ag"][:, u0 * K : (u0 + n) * K],
            )

        def stage1(J, units):
            if units[0] == 0:
                st[J]["z"] = [psum.tile([P, K], F32, name="z%d" % h, bufs=1) for h in range(2)]
            for h in range(2):
                for u in units:
                    cols = slice(u * P, (u + 1) * P)
                    if u == 0:
                        rhs = deep_codes[:, h * K : (h + 1) * K].bitcast(FP8X4)
                        rs = deep_scales[:, h * K : (h + 1) * K]
                    else:
                        rhs = ew[:, u - 1, h * 2 * K : (h + 1) * 2 * K].bitcast(FP4X4)
                        rs = es[:, u - 1, h * K : (h + 1) * K]
                    nc.tensor.matmul_mx(
                        out=st[J]["z"][h][:],
                        lhsT=st[J]["ac"][:, cols].bitcast(FP8X4),
                        lhsT_scale=st[J]["as"][:, cols],
                        rhs=rhs,
                        rhs_scale=rs,
                        start=(u == 0),
                        stop=(u == 4),
                    )

        def relu(J):
            st[J]["cam"] = work.tile([P, S], BF16, name="cam", align_bytes=64)
            for h in range(2):
                nc.scalar.activation(
                    out=st[J]["cam"][:, h * K : (h + 1) * K].rearrange("m (u q e) -> m u q e", u=2, e=2),
                    in_=st[J]["z"][h][:].rearrange("m (q u e) -> m u q e", u=2, e=2),
                    func=RELU,
                )

        def cam_transposes(J):
            tr = psum.tile([P, K], F32, name="b", bufs=6)
            words = st[J]["cam"][:].bitcast(F32)
            for i in range(4):
                nc.tensor.transpose(tr[:, i * P : (i + 1) * P], words[:, i * P : (i + 1) * P], ident[:])
            st[J]["ct"] = tr

        def empty_cam(J):
            st[J]["cg"] = work.tile([P, S], BF16, name="cg", align_bytes=64)
            nc.scalar.copy(
                out=st[J]["cg"][:].bitcast(F32).rearrange("p (c m v) -> p c m v", c=2, v=2),
                in_=st[J]["ct"][:].rearrange("p (c v m) -> p c m v", c=2, v=2),
            )

        def quantize_cam(J):
            st[J]["cc"] = work.tile([P, GS * P], U32, name="cc", align_bytes=64)
            st[J]["cs"] = work.tile([P, GS * P], U8, name="cs", align_bytes=64)
            nc.vector.quantize_mx(out=st[J]["cc"][:].bitcast(FP8X4), scales=st[J]["cs"][:], in_=st[J]["cg"][:])

        def stage2(J, n):
            o = psum.tile([P, 512], F32, name="b", bufs=6)
            for g in range(GS):
                nc.tensor.matmul_mx(
                    out=o[:],
                    lhsT=st[J]["cc"][:, g * P : (g + 1) * P].bitcast(FP8X4),
                    lhsT_scale=st[J]["cs"][:, g * P : (g + 1) * P],
                    rhs=uw[n // 4][:, g, (n % 4) * 1024 : (n % 4 + 1) * 1024].bitcast(FP4X4),
                    rhs_scale=us[:, g, n * 512 : (n + 1) * 512],
                    start=(g == 0),
                    stop=(g == GS - 1),
                )
            if n % 4 == 0:
                st[J]["o"] = outs.tile([P, 2048], F32, name="ot")
            dst = st[J]["o"][:, (n % 4) * 512 : (n % 4 + 1) * 512]
            if (J == JT - 1 or (J == JT - 2 and n > 4)) and n % 2 == 1:
                nc.vector.tensor_copy(out=dst, in_=o[:])
            else:
                nc.scalar.copy(out=dst, in_=o[:])
            w = 4 if J < 2 else 2 if J < 3 or n < 6 else 1
            if n % w == w - 1:
                lo = (n % 4 + 1 - w) * 512
                nc.sync.dma_start(
                    out=out_view[J][:, (n + 1 - w) * 512 : (n + 1) * 512], in_=st[J]["o"][:, lo : lo + w * 512]
                )

        def back(J, count):
            for n in range(st[J]["n"], st[J]["n"] + count):
                stage2(J, n)
            st[J]["n"] += count

        def halves(J, us_):
            for u in us_:
                sum_part(J, u, (0, 1))

        def finish(J, us_):
            for u in us_:
                sum_part(J, u, (2, 3))
                empty_sum(J, u)

        begin(0)
        sum_cells(0, 0)
        deep_copies()
        quantize_a(0, 0)
        quantize_deep(0)
        halves(0, (1, 2, 3, 4))
        finish(0, (1, 2))
        quantize_deep(1)
        quantize_a(0, 1)
        finish(0, (3, 4))
        stage1(0, (0,))
        quantize_a(0, 2)
        stage1(0, (1, 2))
        stage1(0, (3, 4))
        relu(0)
        load_ge(3, 0)
        load_ge(3, 1)
        begin(1)
        sum_cells(1, 0)
        quantize_a(1, 0)
        cam_transposes(0)
        empty_cam(0)
        quantize_cam(0)
        halves(1, (1, 2, 3, 4))
        finish(1, (1, 2))
        quantize_a(1, 1)
        finish(1, (3, 4))
        quantize_a(1, 2)
        stage1(1, (0,))
        stage1(1, (1, 2))
        stage1(1, (3, 4))
        relu(1)
        back(0, 2)
        begin(2)
        sum_cells(2, 0)
        quantize_a(2, 0)
        cam_transposes(1)
        empty_cam(1)
        quantize_cam(1)
        back(0, 2)
        stage1(2, (0,))
        back(1, 4)
        back(0, 4)
        for u in (1, 2, 3, 4):
            sum_cells(2, u)
            if u % 2 == 0:
                quantize_a(2, u // 2)
        begin(3)
        sum_cells(3, 0)
        quantize_a(3, 0)
        back(1, 2)
        stage1(2, (1, 2))
        stage1(2, (3, 4))
        relu(2)
        sum_cells(3, 1)
        sum_cells(3, 2)
        back(1, 2)
        cam_transposes(2)
        empty_cam(2)
        quantize_a(3, 1)
        quantize_cam(2)
        sum_cells(3, 3)
        sum_cells(3, 4)
        quantize_a(3, 2)
        stage1(3, (0,))
        stage1(3, (1, 2))
        back(2, 2)
        stage1(3, (3, 4))
        relu(3)
        back(2, 4)
        cam_transposes(3)
        empty_cam(3)
        quantize_cam(3)
        back(2, 2)
        back(3, 8)
